import numpy as np
import ml_dtypes


def mxq(x, axis, fmt="e4m3"):
    dtype, down = {"e4m3": (ml_dtypes.float8_e4m3fn, 7), "e5m2": (ml_dtypes.float8_e5m2, 14)}[fmt]
    v = np.moveaxis(np.asarray(x, np.float32).astype(ml_dtypes.bfloat16).astype(np.float64), axis, -1)
    blocks = v.reshape(v.shape[:-1] + (-1, 32))
    amax = np.abs(blocks).max(-1, keepdims=True)
    byte = np.maximum(np.where(amax > 0, np.frexp(amax)[1] - 1 + 127, 0) - down, 1)
    scale = np.exp2(byte - 127.0)
    codes = (blocks / scale).astype(np.float32).astype(dtype).astype(np.float64)
    return np.moveaxis((codes * scale).reshape(v.shape), -1, axis)


WIDE = False


def mx_kscale(k):
    if not WIDE:
        return np.ones(k)
    levels = np.array([10, -10, 5, -5, 0])
    if k % 512:
        return np.exp2(np.random.permutation(np.resize(levels, k // 32))).repeat(32)
    a = np.empty((k // 512, 16))
    for p in range(k // 512):
        a[p, :8] = np.random.permutation(np.resize(levels, 8))
        for g in range(8):
            far = levels[np.abs(levels - a[p, g]) >= 10]
            a[p, g + 8] = far[np.random.randint(len(far))]
    return np.exp2(a.ravel()).repeat(32)


def f64(x):
    return np.asarray(x).astype(np.float64)


def striped(idx):
    return np.tile(idx.reshape(-1, 16).T, (8, 1)).astype(np.uint16)


def unstriped(offs):
    return offs[:16].T.reshape(-1).astype(np.int64)


def striped8(idx):
    return np.concatenate([x.reshape(-1, 16).T for x in idx]).astype(np.uint16)


def runs(offs, k):
    lists = np.stack([offs[16 * r : 16 * r + 16].T.reshape(-1) for r in range(8)]).astype(np.int64)
    return lists[np.arange(k) % 512 // 64]


def pack_weight(w):
    k, n = w.shape
    w = f64(np.asarray(w, np.float32).astype(ml_dtypes.bfloat16)).reshape(k // 32, 32, n)
    amax = np.abs(w).max(1)
    byte = np.clip(np.where(amax > 0, np.frexp(amax)[1] - 1 + 127 - 7, 1), 1, 254)
    scaled = (w * np.exp2(127.0 - byte)[:, None, :]).reshape(k, n).astype(np.float32)
    words = np.ascontiguousarray(scaled.reshape(k // 512, 128, 4, n).transpose(0, 1, 3, 2)).astype(ml_dtypes.float8_e4m3fn).view(np.uint8)
    return words, np.ascontiguousarray(byte.astype(np.uint8).reshape(k // 512, 16, n))


def unpack_weight(words, scales):
    g, p, n, _ = words.shape
    vals = np.ascontiguousarray(words).view(ml_dtypes.float8_e4m3fn).astype(np.float64) * np.repeat(np.exp2(scales.astype(np.float64) - 127.0), 8, axis=1)[..., None]
    return vals.transpose(0, 1, 3, 2).reshape(g * 512, n)


def sigmoid(v):
    return 1.0 / (1.0 + np.exp(-np.maximum(v, -700.0)))


K, T, S, N, G, H = 512, 2048, 256, 512, 2048, 512


def setup_inputs():
    n = np.random.standard_normal
    s = mx_kscale(K)[:, None]
    u = mx_kscale(K)
    packed_xT = pack_weight(n((K, T)) * s)
    packed_dT = pack_weight(n((K, G)) / s)
    packed_w1 = pack_weight(n((H, N)) / np.sqrt(2 * H) / u[:, None])
    packed_w2 = pack_weight(n((K, N)) / np.sqrt(2 * K) / s)
    return {
        "x_words": packed_xT[0],
        "x_scales": packed_xT[1],
        "d_words": packed_dT[0],
        "d_scales": packed_dT[1],
        "gn": (np.random.uniform(0.5, 1.5, (H, 1)) * u[:, None]).astype(np.float32),
        "w1_words": packed_w1[0],
        "w1_scales": packed_w1[1],
        "w2_words": packed_w2[0],
        "w2_scales": packed_w2[1],
        "sl": np.random.uniform(1.0, 2.0, (N, 1)).astype(np.float32),
        "th": (0.5 * n((N, 1))).astype(np.float32),
        "offs": striped(np.random.permutation(T)[:S]),
        "k1": striped8(np.random.randint(0, G, (8, H))),
        "two": striped(np.random.permutation(T)[:S]),
        "n1": striped(np.random.permutation(S)),
        "n2": striped(np.random.permutation(S)),
    }


def reference(x_words, x_scales, d_words, d_scales, gn, w1_words, w1_scales, w2_words, w2_scales, sl, th, offs, k1, two, n1, n2):
    d_k1 = unpack_weight(d_words, d_scales)[np.arange(K)[:, None], runs(k1, K)]
    xq = unpack_weight(x_words, x_scales)[:, unstriped(offs)]
    s = 0.0625 * (d_k1.T @ xq)
    z = f64(gn) * s
    x_two = unpack_weight(x_words, x_scales)[:, unstriped(two)]
    h = unpack_weight(w1_words, w1_scales).T @ mxq(z, 0, "e4m3") + unpack_weight(w2_words, w2_scales).T @ x_two
    ds = np.zeros((N, S))
    ds[:, unstriped(n1)] = h
    sg = sigmoid(f64(sl) * (ds[:, unstriped(n2)] - f64(th)))
    return h * sg

@@ -1,0 +1,219 @@
+from contextlib import ExitStack
+
+import concourse.mybir as mybir
+
+K, T, S, N, G, H = 512, 2048, 256, 512, 2048, 512
+FLOPS = 2 * K * H * S + 2 * H * N * S + 2 * K * N * S
+
+F32 = mybir.dt.float32
+BF16 = mybir.dt.bfloat16
+I32 = mybir.dt.int32
+U32 = mybir.dt.uint32
+U16 = mybir.dt.uint16
+U8 = mybir.dt.uint8
+FP8X4 = mybir.dt.float8_e4m3fn_x4
+MULT = mybir.AluOpType.mult
+COPY = mybir.ActivationFunctionType.Copy
+SIGMOID = mybir.ActivationFunctionType.Sigmoid
+
+P = 128
+PACK = 4
+HALF = S // 2
+X_PLANE = 12
+W_PLANE = 4
+WINDOW = 2 * S
+
+
+def tile_picked_kmixierl_none_p_kernel(
+    tc, x_words, x_scales, d_words, d_scales, gn, w1_words, w1_scales, w2_words, w2_scales, sl, th, offs, k1, two, n1, n2, out
+):
+    nc = tc.nc
+
+    def words_view(dram):
+        return dram[0].rearrange("p n t -> p (n t)").bitcast(I32)
+
+    def entries(list_tile, first, count):
+        return list_tile[:, first // 16 : (first + count) // 16]
+
+    with ExitStack() as ctx:
+        sb = ctx.enter_context(tc.tile_pool(name="sb", bufs=1))
+        ps = ctx.enter_context(tc.psum_pool(name="ps", bufs=1))
+
+        k1_t = sb.tile([P, H // 16], U16, name="k1_t")
+        offs_t = sb.tile([P, S // 16], U16, name="offs_t")
+        two_t = sb.tile([P, S // 16], U16, name="two_t")
+        n1_t = sb.tile([P, S // 16], U16, name="n1_t")
+        n2_t = sb.tile([P, S // 16], U16, name="n2_t")
+
+        d_scale_table = sb.tile([P, G], U8, name="d_scale_table", align_bytes=64)
+        x_scale_table = sb.tile([P, T], U8, name="x_scale_table", align_bytes=64)
+        d_table = sb.tile([P, G], U32, name="d_table", align_bytes=64)
+        x_table = sb.tile([P, T], U32, name="x_table", align_bytes=64)
+        planes = sb.tile([P, H + 2 * N], U8, name="planes", align_bytes=64)
+        w1_t = sb.tile([P, N], U32, name="w1_t", align_bytes=64)
+        w2_t = sb.tile([P, N], U32, name="w2_t", align_bytes=64)
+        gn_t = sb.tile([P, PACK], F32, name="gn_t")
+        sl_t = sb.tile([P, N // P], F32, name="sl_t")
+        th_t = sb.tile([P, N // P], F32, name="th_t")
+        bias_t = sb.tile([P, N // P], F32, name="bias_t")
+
+        planes32 = planes[:].bitcast(I32)
+        w1_col, w2_col = H, H + N
+
+        nc.vector.memset(planes32[:, w1_col // 4 :], 0)
+        nc.vector.memset(d_scale_table[:].bitcast(I32), 0)
+        nc.vector.memset(x_scale_table[:].bitcast(I32), 0)
+
+        nc.sync.dma_start(k1_t[:], k1)
+        nc.sync.dma_start(offs_t[:], offs)
+        nc.sync.dma_start(planes32[0:P:8, w1_col // 4 : w2_col // 4], w1_scales[0].bitcast(I32))
+        nc.sync.dma_start(planes32[0:P:8, w2_col // 4 :], w2_scales[0].bitcast(I32))
+        nc.sync.dma_start(d_scale_table[:].bitcast(I32)[0:P:8, :], d_scales[0].bitcast(I32))
+        nc.sync.dma_start(d_table[:].bitcast(I32), words_view(d_words))
+        for q in range(4):
+            nc.sync.dma_start(
+                x_scale_table[:].bitcast(I32)[32 * q + X_PLANE : 32 * q + X_PLANE + 4, :],
+                x_scales[0].bitcast(I32)[4 * q : 4 * q + 4, :],
+            )
+        nc.sync.dma_start(gn_t[:], gn.rearrange("(p t) o -> p (t o)", t=PACK))
+        nc.sync.dma_start(x_table[:].bitcast(I32), words_view(x_words))
+        nc.sync.dma_start(two_t[:], two)
+
+        key_scales = sb.tile([P, H], U8, name="key_scales", align_bytes=64)
+        nc.vector.tensor_copy(key_scales[:], d_scale_table[:].indirect(k1_t[:]))
+        nc.vector.tensor_copy(
+            planes[:, 0:H].rearrange("p (t m) -> p m t", t=PACK),
+            key_scales[:].rearrange("p (m t) -> p m t", t=PACK),
+        )
+        for q in range(4):
+            nc.sync.dma_start(
+                planes32[32 * q + W_PLANE : 32 * q + W_PLANE + 4, :], planes32[32 * q : 32 * q + 32 : 8, :]
+            )
+
+        nc.sync.dma_start(w2_t[:].bitcast(I32), words_view(w2_words))
+        nc.sync.dma_start(w1_t[:].bitcast(I32), words_view(w1_words))
+        nc.sync.dma_start(n1_t[:], n1)
+        nc.sync.dma_start(n2_t[:], n2)
+        with nc.allow_non_contiguous_dma(reason="one float32 a partition for each tile of output rows"):
+            nc.sync.dma_start(sl_t[:], sl.rearrange("(t p) o -> p (t o)", p=P))
+            nc.sync.dma_start(th_t[:], th.rearrange("(t p) o -> p (t o)", p=P))
+
+        key_words = sb.tile([P, H], U32, name="key_words", align_bytes=64)
+        keys = sb.tile([P, H], U32, name="keys", align_bytes=64)
+        nc.vector.tensor_copy(key_words[:], d_table[:].indirect(k1_t[:]))
+        nc.vector.tensor_copy(
+            keys[:].rearrange("p (t m) -> p m t", t=PACK),
+            key_words[:].rearrange("p (m t) -> p m t", t=PACK),
+        )
+
+        xq_scales = sb.tile([P, S], U8, name="xq_scales", align_bytes=64)
+        nc.vector.tensor_copy(xq_scales[:], x_scale_table[:].indirect(offs_t[:]))
+
+        halves = [slice(0, HALF), slice(HALF, S)]
+        xq = sb.tile([P, S], U32, name="xq", tag="picked_words", align_bytes=64)
+        for c in halves:
+            nc.vector.tensor_copy(xq[:, c], x_table[:].indirect(entries(offs_t, c.start, HALF)))
+        x2_scales = sb.tile([P, S], U8, name="x2_scales", align_bytes=64)
+        nc.vector.tensor_copy(x2_scales[:], x_scale_table[:].indirect(two_t[:]))
+
+        scores = [ps.tile([P, PACK, HALF], F32, name=f"scores{a}") for a in range(2)]
+        for a, c in enumerate(halves):
+            for t in range(PACK):
+                nc.tensor.matmul_mx(
+                    out=scores[a][:, t, :],
+                    lhsT=keys[:, t * P : (t + 1) * P].bitcast(FP8X4),
+                    lhsT_scale=planes[W_PLANE:P, t * P : (t + 1) * P],
+                    rhs=xq[:, c].bitcast(FP8X4),
+                    rhs_scale=xq_scales[X_PLANE:P, c],
+                    start=True,
+                    stop=True,
+                )
+
+        z = [sb.tile([P, HALF, PACK], BF16, name=f"z{a}", align_bytes=64) for a in range(2)]
+        zq = sb.tile([P, S], U32, name="zq", align_bytes=64)
+        zq_scales = sb.tile([P, S], U8, name="zq_scales", align_bytes=64)
+        x2 = sb.tile([P, S], U32, name="x2", tag="picked_words", align_bytes=64)
+        for a, c in enumerate(halves):
+            nc.vector.scalar_tensor_tensor(
+                out=z[a][:],
+                in0=scores[a][:].rearrange("p t j -> p j t"),
+                scalar=0.0625,
+                in1=gn_t[:].unsqueeze(1).to_broadcast([P, HALF, PACK]),
+                op0=MULT,
+                op1=MULT,
+            )
+            nc.vector.tensor_copy(x2[:, c], x_table[:].indirect(entries(two_t, c.start, HALF)))
+            nc.vector.quantize_mx(
+                out=zq[:, c].bitcast(FP8X4), scales=zq_scales[:, c], in_=z[a][:].rearrange("p j t -> p (j t)")
+            )
+
+        def h_products(bank, m, c):
+            rows = slice(m * P, (m + 1) * P)
+            nc.tensor.matmul_mx(
+                out=bank,
+                lhsT=w2_t[:, rows].bitcast(FP8X4),
+                lhsT_scale=planes[W_PLANE:P, w2_col + m * P : w2_col + (m + 1) * P],
+                rhs=x2[:, c].bitcast(FP8X4),
+                rhs_scale=x2_scales[X_PLANE:P, c],
+                start=True,
+                stop=False,
+            )
+            nc.tensor.matmul_mx(
+                out=bank,
+                lhsT=w1_t[:, rows].bitcast(FP8X4),
+                lhsT_scale=planes[W_PLANE:P, w1_col + m * P : w1_col + (m + 1) * P],
+                rhs=zq[:, c].bitcast(FP8X4),
+                rhs_scale=zq_scales[:, c],
+                start=False,
+                stop=True,
+            )
+
+        h01 = sb.tile([P, 2, S], F32, name="h01")
+        h23 = sb.tile([P, 2, S], F32, name="h23")
+        h = [h01[:, 0, :], h01[:, 1, :], h23[:, 0, :], h23[:, 1, :]]
+        ds = [sb.tile([P, WINDOW], F32, name=f"ds{m}") for m in range(4)]
+        sg = [sb.tile([P, S], F32, name=f"sg{m}") for m in range(4)]
+        res = [sb.tile([P, S], F32, name=f"res{m}") for m in range(4)]
+
+        def scatter(m, c):
+            nc.scalar.activation(ds[m][:].indirect(entries(n1_t, c.start, c.stop - c.start)), h[m][:, c], COPY)
+
+        def finish(m, c):
+            nc.scalar.activation(
+                sg[m][:, c],
+                ds[m][:].indirect(entries(n2_t, c.start, c.stop - c.start)),
+                SIGMOID,
+                bias=bias_t[:, m : m + 1],
+                scale=sl_t[:, m : m + 1],
+            )
+            nc.vector.tensor_tensor(res[m][:, c], h[m][:, c], sg[m][:, c], MULT)
+            nc.sync.dma_start(out[m * P : (m + 1) * P, c], res[m][:, c])
+
+        first, second, whole = halves[0], halves[1], slice(0, S)
+        bank0 = ps.tile([P, HALF], F32, name="bank0")
+        bank1 = ps.tile([P, HALF], F32, name="bank1")
+        bank01 = ps.tile([P, 2, HALF], F32, name="bank01")
+        bank23 = ps.tile([P, 2, S], F32, name="bank23")
+
+        h_products(bank0[:], 0, first)
+        nc.scalar.copy(h[0][:, first], bank0[:])
+        scatter(0, first)
+        h_products(bank1[:], 1, first)
+        nc.vector.tensor_copy(h[1][:, first], bank1[:])
+        scatter(1, first)
+        for m in range(2):
+            h_products(bank01[:, m, :], m, second)
+        nc.vector.tensor_copy(h01[:, :, second], bank01[:])
+        for m in range(2):
+            scatter(m, second)
+        for m in range(2):
+            h_products(bank23[:, m, :], 2 + m, whole)
+        nc.vector.tensor_copy(h23[:], bank23[:])
+        nc.vector.scalar_tensor_tensor(out=bias_t[:], in0=th_t[:], scalar=-1.0, in1=sl_t[:], op0=MULT, op1=MULT)
+        finish(0, whole)
+        finish(1, whole)
+        for m in (2, 3):
+            scatter(m, whole)
+        finish(2, whole)
+        for c in halves:
+            finish(3, c)

@@ -76,6 +76,8 @@ def tile_picked_kmixierl_none_p_kernel(
                 x_scales[0].bitcast(I32)[4 * q : 4 * q + 4, :],
             )
         nc.sync.dma_start(gn_t[:], gn.rearrange("(p t) o -> p (t o)", t=PACK))
+        warm = sb.tile([P, 1], F32, name="warm")
+        nc.scalar.activation(warm[:], gn_t[:, 0:1], SIGMOID)
         nc.sync.dma_start(x_table[:].bitcast(I32), words_view(x_words))
         nc.sync.dma_start(two_t[:], two)
 

@@ -79,7 +79,6 @@ def tile_picked_kmixierl_none_p_kernel(
         warm = sb.tile([P, 1], F32, name="warm")
         nc.scalar.activation(warm[:], gn_t[:, 0:1], SIGMOID)
         nc.sync.dma_start(x_table[:].bitcast(I32), words_view(x_words))
-        nc.sync.dma_start(two_t[:], two)
 
         key_scales = sb.tile([P, H], U8, name="key_scales", align_bytes=64)
         nc.vector.tensor_copy(key_scales[:], d_scale_table[:].indirect(k1_t[:]))
@@ -92,6 +91,7 @@ def tile_picked_kmixierl_none_p_kernel(
                 planes32[32 * q + W_PLANE : 32 * q + W_PLANE + 4, :], planes32[32 * q : 32 * q + 32 : 8, :]
             )
 
+        nc.sync.dma_start(two_t[:], two)
         nc.sync.dma_start(w2_t[:].bitcast(I32), words_view(w2_words))
         nc.sync.dma_start(w1_t[:].bitcast(I32), words_view(w1_words))
         nc.sync.dma_start(n1_t[:], n1)
@@ -131,13 +131,13 @@ def tile_picked_kmixierl_none_p_kernel(
                     stop=True,
                 )
 
-        z = [sb.tile([P, HALF, PACK], BF16, name=f"z{a}", align_bytes=64) for a in range(2)]
         zq = sb.tile([P, S], U32, name="zq", align_bytes=64)
         zq_scales = sb.tile([P, S], U8, name="zq_scales", align_bytes=64)
         x2 = sb.tile([P, S], U32, name="x2", tag="picked_words", align_bytes=64)
         for a, c in enumerate(halves):
+            z = sb.tile([P, HALF, PACK], BF16, name="z", align_bytes=64)
             nc.vector.scalar_tensor_tensor(
-                out=z[a][:],
+                out=z[:],
                 in0=scores[a][:].rearrange("p t j -> p j t"),
                 scalar=0.0625,
                 in1=gn_t[:].unsqueeze(1).to_broadcast([P, HALF, PACK]),
@@ -146,7 +146,7 @@ def tile_picked_kmixierl_none_p_kernel(
             )
             nc.vector.tensor_copy(x2[:, c], x_table[:].indirect(entries(two_t, c.start, HALF)))
             nc.vector.quantize_mx(
-                out=zq[:, c].bitcast(FP8X4), scales=zq_scales[:, c], in_=z[a][:].rearrange("p j t -> p (j t)")
+                out=zq[:, c].bitcast(FP8X4), scales=zq_scales[:, c], in_=z[:].rearrange("p j t -> p (j t)")
             )
 
         def h_products(bank, m, c):

@@ -64,21 +64,23 @@ def tile_picked_kmixierl_none_p_kernel(
         nc.vector.memset(d_scale_table[:].bitcast(I32), 0)
         nc.vector.memset(x_scale_table[:].bitcast(I32), 0)
 
+        nc.sync.dma_start(d_table[:].bitcast(I32)[:, : 3 * G // 8], words_view(d_words)[:, : 3 * G // 8])
         nc.sync.dma_start(k1_t[:], k1)
-        nc.sync.dma_start(offs_t[:], offs)
         nc.sync.dma_start(planes32[0:P:8, w1_col // 4 : w2_col // 4], w1_scales[0].bitcast(I32))
         nc.sync.dma_start(planes32[0:P:8, w2_col // 4 :], w2_scales[0].bitcast(I32))
         nc.sync.dma_start(d_scale_table[:].bitcast(I32)[0:P:8, :], d_scales[0].bitcast(I32))
-        nc.sync.dma_start(d_table[:].bitcast(I32), words_view(d_words))
+        nc.sync.dma_start(d_table[:].bitcast(I32)[:, 3 * G // 8 :], words_view(d_words)[:, 3 * G // 8 :])
+        nc.sync.dma_start(gn_t[:], gn.rearrange("(p t) o -> p (t o)", t=PACK))
+        nc.sync.dma_start(offs_t[:], offs)
         for q in range(4):
             nc.sync.dma_start(
                 x_scale_table[:].bitcast(I32)[32 * q + X_PLANE : 32 * q + X_PLANE + 4, :],
                 x_scales[0].bitcast(I32)[4 * q : 4 * q + 4, :],
             )
-        nc.sync.dma_start(gn_t[:], gn.rearrange("(p t) o -> p (t o)", t=PACK))
         warm = sb.tile([P, 1], F32, name="warm")
         nc.scalar.activation(warm[:], gn_t[:, 0:1], SIGMOID)
         nc.sync.dma_start(x_table[:].bitcast(I32), words_view(x_words))
+        nc.sync.dma_start(two_t[:], two)
 
         key_scales = sb.tile([P, H], U8, name="key_scales", align_bytes=64)
         nc.vector.tensor_copy(key_scales[:], d_scale_table[:].indirect(k1_t[:]))
@@ -91,7 +93,6 @@ def tile_picked_kmixierl_none_p_kernel(
                 planes32[32 * q + W_PLANE : 32 * q + W_PLANE + 4, :], planes32[32 * q : 32 * q + 32 : 8, :]
             )
 
-        nc.sync.dma_start(two_t[:], two)
         nc.sync.dma_start(w2_t[:].bitcast(I32), words_view(w2_words))
         nc.sync.dma_start(w1_t[:].bitcast(I32), words_view(w1_words))
         nc.sync.dma_start(n1_t[:], n1)

from contextlib import ExitStack

import concourse.mybir as mybir

K, T, S, N, G, H = 512, 2048, 256, 512, 2048, 512
FLOPS = 2 * K * H * S + 2 * H * N * S + 2 * K * N * S

F32 = mybir.dt.float32
BF16 = mybir.dt.bfloat16
I32 = mybir.dt.int32
U32 = mybir.dt.uint32
U16 = mybir.dt.uint16
U8 = mybir.dt.uint8
FP8X4 = mybir.dt.float8_e4m3fn_x4
MULT = mybir.AluOpType.mult
COPY = mybir.ActivationFunctionType.Copy
SIGMOID = mybir.ActivationFunctionType.Sigmoid

P = 128
PACK = 4
HALF = S // 2
X_PLANE = 12
W_PLANE = 4
WINDOW = 2 * S


def tile_picked_kmixierl_none_p_kernel(
    tc, x_words, x_scales, d_words, d_scales, gn, w1_words, w1_scales, w2_words, w2_scales, sl, th, offs, k1, two, n1, n2, out
):
    nc = tc.nc

    def words_view(dram):
        return dram[0].rearrange("p n t -> p (n t)").bitcast(I32)

    def entries(list_tile, first, count):
        return list_tile[:, first // 16 : (first + count) // 16]

    with ExitStack() as ctx:
        sb = ctx.enter_context(tc.tile_pool(name="sb", bufs=1))
        ps = ctx.enter_context(tc.psum_pool(name="ps", bufs=1))

        k1_t = sb.tile([P, H // 16], U16, name="k1_t")
        offs_t = sb.tile([P, S // 16], U16, name="offs_t")
        two_t = sb.tile([P, S // 16], U16, name="two_t")
        n1_t = sb.tile([P, S // 16], U16, name="n1_t")
        n2_t = sb.tile([P, S // 16], U16, name="n2_t")

        d_scale_table = sb.tile([P, G], U8, name="d_scale_table", align_bytes=64)
        x_scale_table = sb.tile([P, T], U8, name="x_scale_table", align_bytes=64)
        d_table = sb.tile([P, G], U32, name="d_table", align_bytes=64)
        x_table = sb.tile([P, T], U32, name="x_table", align_bytes=64)
        planes = sb.tile([P, H + 2 * N], U8, name="planes", align_bytes=64)
        w1_t = sb.tile([P, N], U32, name="w1_t", align_bytes=64)
        w2_t = sb.tile([P, N], U32, name="w2_t", align_bytes=64)
        gn_t = sb.tile([P, PACK], F32, name="gn_t")
        sl_t = sb.tile([P, N // P], F32, name="sl_t")
        th_t = sb.tile([P, N // P], F32, name="th_t")
        bias_t = sb.tile([P, N // P], F32, name="bias_t")

        planes32 = planes[:].bitcast(I32)
        w1_col, w2_col = H, H + N

        nc.vector.memset(planes32[:, w1_col // 4 :], 0)
        nc.vector.memset(d_scale_table[:].bitcast(I32), 0)
        nc.vector.memset(x_scale_table[:].bitcast(I32), 0)

        nc.sync.dma_start(d_table[:].bitcast(I32)[:, : 3 * G // 8], words_view(d_words)[:, : 3 * G // 8])
        nc.sync.dma_start(k1_t[:], k1)
        nc.sync.dma_start(planes32[0:P:8, w1_col // 4 : w2_col // 4], w1_scales[0].bitcast(I32))
        nc.sync.dma_start(planes32[0:P:8, w2_col // 4 :], w2_scales[0].bitcast(I32))
        nc.sync.dma_start(d_scale_table[:].bitcast(I32)[0:P:8, :], d_scales[0].bitcast(I32))
        nc.sync.dma_start(d_table[:].bitcast(I32)[:, 3 * G // 8 :], words_view(d_words)[:, 3 * G // 8 :])
        nc.sync.dma_start(gn_t[:], gn.rearrange("(p t) o -> p (t o)", t=PACK))
        nc.sync.dma_start(offs_t[:], offs)
        for q in range(4):
            nc.sync.dma_start(
                x_scale_table[:].bitcast(I32)[32 * q + X_PLANE : 32 * q + X_PLANE + 4, :],
                x_scales[0].bitcast(I32)[4 * q : 4 * q + 4, :],
            )
        warm = sb.tile([P, 1], F32, name="warm")
        nc.scalar.activation(warm[:], gn_t[:, 0:1], SIGMOID)
        nc.sync.dma_start(x_table[:].bitcast(I32), words_view(x_words))
        nc.sync.dma_start(two_t[:], two)

        key_scales = sb.tile([P, H], U8, name="key_scales", align_bytes=64)
        nc.vector.tensor_copy(key_scales[:], d_scale_table[:].indirect(k1_t[:]))
        nc.vector.tensor_copy(
            planes[:, 0:H].rearrange("p (t m) -> p m t", t=PACK),
            key_scales[:].rearrange("p (m t) -> p m t", t=PACK),
        )
        for q in range(4):
            nc.sync.dma_start(
                planes32[32 * q + W_PLANE : 32 * q + W_PLANE + 4, :], planes32[32 * q : 32 * q + 32 : 8, :]
            )

        nc.sync.dma_start(w2_t[:].bitcast(I32), words_view(w2_words))
        nc.sync.dma_start(w1_t[:].bitcast(I32), words_view(w1_words))
        nc.sync.dma_start(n1_t[:], n1)
        nc.sync.dma_start(n2_t[:], n2)
        with nc.allow_non_contiguous_dma(reason="one float32 a partition for each tile of output rows"):
            nc.sync.dma_start(sl_t[:], sl.rearrange("(t p) o -> p (t o)", p=P))
            nc.sync.dma_start(th_t[:], th.rearrange("(t p) o -> p (t o)", p=P))

        key_words = sb.tile([P, H], U32, name="key_words", align_bytes=64)
        keys = sb.tile([P, H], U32, name="keys", align_bytes=64)
        nc.vector.tensor_copy(key_words[:], d_table[:].indirect(k1_t[:]))
        nc.vector.tensor_copy(
            keys[:].rearrange("p (t m) -> p m t", t=PACK),
            key_words[:].rearrange("p (m t) -> p m t", t=PACK),
        )

        xq_scales = sb.tile([P, S], U8, name="xq_scales", align_bytes=64)
        nc.vector.tensor_copy(xq_scales[:], x_scale_table[:].indirect(offs_t[:]))

        halves = [slice(0, HALF), slice(HALF, S)]
        xq = sb.tile([P, S], U32, name="xq", tag="picked_words", align_bytes=64)
        for c in halves:
            nc.vector.tensor_copy(xq[:, c], x_table[:].indirect(entries(offs_t, c.start, HALF)))
        x2_scales = sb.tile([P, S], U8, name="x2_scales", align_bytes=64)
        nc.vector.tensor_copy(x2_scales[:], x_scale_table[:].indirect(two_t[:]))

        scores = [ps.tile([P, PACK, HALF], F32, name=f"scores{a}") for a in range(2)]
        for a, c in enumerate(halves):
            for t in range(PACK):
                nc.tensor.matmul_mx(
                    out=scores[a][:, t, :],
                    lhsT=keys[:, t * P : (t + 1) * P].bitcast(FP8X4),
                    lhsT_scale=planes[W_PLANE:P, t * P : (t + 1) * P],
                    rhs=xq[:, c].bitcast(FP8X4),
                    rhs_scale=xq_scales[X_PLANE:P, c],
                    start=True,
                    stop=True,
                )

        zq = sb.tile([P, S], U32, name="zq", align_bytes=64)
        zq_scales = sb.tile([P, S], U8, name="zq_scales", align_bytes=64)
        x2 = sb.tile([P, S], U32, name="x2", tag="picked_words", align_bytes=64)
        for a, c in enumerate(halves):
            z = sb.tile([P, HALF, PACK], BF16, name="z", align_bytes=64)
            nc.vector.scalar_tensor_tensor(
                out=z[:],
                in0=scores[a][:].rearrange("p t j -> p j t"),
                scalar=0.0625,
                in1=gn_t[:].unsqueeze(1).to_broadcast([P, HALF, PACK]),
                op0=MULT,
                op1=MULT,
            )
            nc.vector.tensor_copy(x2[:, c], x_table[:].indirect(entries(two_t, c.start, HALF)))
            nc.vector.quantize_mx(
                out=zq[:, c].bitcast(FP8X4), scales=zq_scales[:, c], in_=z[:].rearrange("p j t -> p (j t)")
            )

        def h_products(bank, m, c):
            rows = slice(m * P, (m + 1) * P)
            nc.tensor.matmul_mx(
                out=bank,
                lhsT=w2_t[:, rows].bitcast(FP8X4),
                lhsT_scale=planes[W_PLANE:P, w2_col + m * P : w2_col + (m + 1) * P],
                rhs=x2[:, c].bitcast(FP8X4),
                rhs_scale=x2_scales[X_PLANE:P, c],
                start=True,
                stop=False,
            )
            nc.tensor.matmul_mx(
                out=bank,
                lhsT=w1_t[:, rows].bitcast(FP8X4),
                lhsT_scale=planes[W_PLANE:P, w1_col + m * P : w1_col + (m + 1) * P],
                rhs=zq[:, c].bitcast(FP8X4),
                rhs_scale=zq_scales[:, c],
                start=False,
                stop=True,
            )

        h01 = sb.tile([P, 2, S], F32, name="h01")
        h23 = sb.tile([P, 2, S], F32, name="h23")
        h = [h01[:, 0, :], h01[:, 1, :], h23[:, 0, :], h23[:, 1, :]]
        ds = [sb.tile([P, WINDOW], F32, name=f"ds{m}") for m in range(4)]
        sg = [sb.tile([P, S], F32, name=f"sg{m}") for m in range(4)]
        res = [sb.tile([P, S], F32, name=f"res{m}") for m in range(4)]

        def scatter(m, c):
            nc.scalar.activation(ds[m][:].indirect(entries(n1_t, c.start, c.stop - c.start)), h[m][:, c], COPY)

        def finish(m, c):
            nc.scalar.activation(
                sg[m][:, c],
                ds[m][:].indirect(entries(n2_t, c.start, c.stop - c.start)),
                SIGMOID,
                bias=bias_t[:, m : m + 1],
                scale=sl_t[:, m : m + 1],
            )
            nc.vector.tensor_tensor(res[m][:, c], h[m][:, c], sg[m][:, c], MULT)
            nc.sync.dma_start(out[m * P : (m + 1) * P, c], res[m][:, c])

        first, second, whole = halves[0], halves[1], slice(0, S)
        bank0 = ps.tile([P, HALF], F32, name="bank0")
        bank1 = ps.tile([P, HALF], F32, name="bank1")
        bank01 = ps.tile([P, 2, HALF], F32, name="bank01")
        bank23 = ps.tile([P, 2, S], F32, name="bank23")

        h_products(bank0[:], 0, first)
        nc.scalar.copy(h[0][:, first], bank0[:])
        scatter(0, first)
        h_products(bank1[:], 1, first)
        nc.vector.tensor_copy(h[1][:, first], bank1[:])
        scatter(1, first)
        for m in range(2):
            h_products(bank01[:, m, :], m, second)
        nc.vector.tensor_copy(h01[:, :, second], bank01[:])
        for m in range(2):
            scatter(m, second)
        for m in range(2):
            h_products(bank23[:, m, :], 2 + m, whole)
        nc.vector.tensor_copy(h23[:], bank23[:])
        nc.vector.scalar_tensor_tensor(out=bias_t[:], in0=th_t[:], scalar=-1.0, in1=sl_t[:], op0=MULT, op1=MULT)
        finish(0, whole)
        finish(1, whole)
        for m in (2, 3):
            scatter(m, whole)
        finish(2, whole)
        for c in halves:
            finish(3, c)
